import numpy as np
import ml_dtypes


def mxq(x, axis, fmt="e4m3"):
    dtype, down = {"e4m3": (ml_dtypes.float8_e4m3fn, 7), "e5m2": (ml_dtypes.float8_e5m2, 14)}[fmt]
    v = np.moveaxis(np.asarray(x, np.float32).astype(ml_dtypes.bfloat16).astype(np.float64), axis, -1)
    blocks = v.reshape(v.shape[:-1] + (-1, 32))
    amax = np.abs(blocks).max(-1, keepdims=True)
    byte = np.maximum(np.where(amax > 0, np.frexp(amax)[1] - 1 + 127, 0) - down, 1)
    scale = np.exp2(byte - 127.0)
    codes = (blocks / scale).astype(np.float32).astype(dtype).astype(np.float64)
    return np.moveaxis((codes * scale).reshape(v.shape), -1, axis)


WIDE = False


def mx_kscale(k):
    if not WIDE:
        return np.ones(k)
    levels = np.array([30, -30])
    if k % 512:
        return np.exp2(np.random.permutation(np.resize(levels, k // 32))).repeat(32)
    a = np.empty((k // 512, 16))
    for p in range(k // 512):
        a[p, :8] = np.random.permutation(np.resize(levels, 8))
        for g in range(8):
            far = levels[np.abs(levels - a[p, g]) >= 10]
            a[p, g + 8] = far[np.random.randint(len(far))]
    return np.exp2(a.ravel()).repeat(32)


BF16 = ml_dtypes.bfloat16


def bf(x):
    return np.asarray(x, np.float32).astype(BF16)


def f64(x):
    return np.asarray(x).astype(np.float64)


H, W = 1024, 1536

TAIL = 0.7
GAIN = 0.1
BACK = 0.3


def setup_inputs():
    s = mx_kscale(H)
    t = mx_kscale(W)
    x = np.random.standard_normal((H, W)) * np.exp(TAIL * np.random.standard_normal((H, W)))
    left = np.random.standard_normal((H, H)) / np.sqrt(H)
    right = np.random.standard_normal((W, W)) / np.sqrt(W)
    return {"x": bf(x * s[:, None] * t),
            "left": bf(left * s[:, None] / s),
            "right": bf(right / t[:, None] * t),
            "row_gain": bf((1 + GAIN * np.random.standard_normal(H)) / s),
            "col_gain": bf((1 + GAIN * np.random.standard_normal(W)) / t),
            "background": bf(BACK * np.random.standard_normal(W))}


def reference(x, left, right, row_gain, col_gain, background):
    img = f64(x)
    vertical = mxq(f64(left), 1, "e4m3") @ mxq(img, 0, "e4m3")
    horizontal = mxq(img, 1, "e5m2") @ mxq(f64(right), 0, "e4m3")
    y = (vertical + horizontal) * f64(row_gain)[:, None] * f64(col_gain)
    return y + f64(background)

@@ -1,0 +1,288 @@
+from contextlib import ExitStack
+
+import concourse.mybir as mybir
+from concourse.masks import make_identity
+
+H, W = 1024, 1536
+FLOPS = 2 * H * H * W + 2 * H * W * W
+
+F32 = mybir.dt.float32
+BF16 = mybir.dt.bfloat16
+U32 = mybir.dt.uint32
+U8 = mybir.dt.uint8
+E4M3 = mybir.dt.float8_e4m3fn_x4
+E5M2 = mybir.dt.float8_e5m2_x4
+ALU = mybir.AluOpType
+
+P = 128
+PACK = 4
+S = P * PACK
+
+
+def tile_additive_sylvester_transform_s2_kernel(tc, x, left, right, row_gain, col_gain, background, out):
+    nc = tc.nc
+    with ExitStack() as ctx:
+        keep = ctx.enter_context(tc.tile_pool(name="keep", bufs=1))
+        stage = ctx.enter_context(tc.tile_pool(name="stage", bufs=8))
+        res = ctx.enter_context(tc.tile_pool(name="res", bufs=12))
+        psum = ctx.enter_context(tc.psum_pool(name="psum", bufs=1))
+        ctx.enter_context(tc.manual_schedule())
+
+        raw, grouped, codes, scales = {}, {}, {}, {}
+
+        def bank(b):
+            return psum.tile([P, S], F32, name="bank%d" % b)
+
+        def load(which, r, c0, c1):
+            src = x if which == "x" else right
+            t = keep.tile([P, PACK, (c1 - c0) * S], BF16, name="raw_%s%d%d" % (which, r, c0), align_bytes=64)
+            nc.sync.dma_start(out=t[:], in_=src[r * S:(r + 1) * S, c0 * S:c1 * S].rearrange("(p j) w -> p j w", j=PACK))
+            for c in range(c0, c1):
+                raw[which, r, c] = t[:, :, (c - c0) * S:(c - c0 + 1) * S]
+
+        def load_left(g, h0, h1):
+            t = keep.tile([P, 2 * (h1 - h0), H], BF16, name="raw_left%d%d" % (g, h0), align_bytes=64)
+            nc.sync.dma_start(out=t[:], in_=left[g * S:(g + 1) * S, :].rearrange("(p j) w -> p j w", j=PACK)[:, 2 * h0:2 * h1, :])
+            for h in range(h0, h1):
+                raw["left", g, h] = t[:, 2 * (h - h0):2 * (h - h0 + 1), :].rearrange("p j (c w) -> p (j c) w", c=2)
+
+        def weave(key, on_vector):
+            g = stage.tile([P, PACK * S], BF16, name="grouped", align_bytes=64)
+            dst = g[:].rearrange("p (c i t) -> p c t i", i=4, t=PACK)
+            src = raw[key[1:]].rearrange("p t (c i) -> p c t i", i=4)
+            cut = on_vector // 4
+            if on_vector > 0:
+                nc.vector.tensor_copy(out=dst[:, :cut], in_=src[:, :cut])
+            if on_vector < S:
+                nc.scalar.copy(out=dst[:, cut:], in_=src[:, cut:])
+            grouped[key] = g
+
+        def turn(key, banks):
+            g = stage.tile([P, PACK * S], BF16, name="grouped", align_bytes=64)
+            words = raw[key[1:]].bitcast(F32)
+            g_words = g[:].bitcast(F32)
+            for half in range(2):
+                pt = bank(banks[half])
+                for jj in range(2):
+                    for u in range(2):
+                        q = 2 * jj + u
+                        nc.tensor.transpose(pt[:, q * P:(q + 1) * P], words[:, 2 * half + jj, u:2 * P:2], ident[:])
+                nc.scalar.copy(
+                    out=g_words[:, half * S:(half + 1) * S].rearrange("p (j r u) -> p j r u", j=2, u=2),
+                    in_=pt[:].rearrange("p (j u r) -> p j r u", j=2, u=2),
+                )
+            grouped[key] = g
+
+        def fmt(key):
+            return E5M2 if key[:2] == ("stationary", "x") else E4M3
+
+        def quantise(key):
+            name = "%s_%s%d%d" % key
+            codes[key] = keep.tile([P, S], U32, name="c_" + name, align_bytes=64)
+            scales[key] = keep.tile([P, S], U8, name="s_" + name, align_bytes=64)
+            nc.vector.quantize_mx(out=codes[key][:].bitcast(fmt(key)), scales=scales[key][:], in_=grouped[key][:])
+
+        passes = [("left", "x", 0), ("x", "right", 0), ("left", "x", 1), ("x", "right", 1), ("x", "right", 2)]
+        acc, scaled = {}, {}
+
+        def moving(n, step):
+            return ("moving", passes[step][1], passes[step][2], n)
+
+        def xt(g, c):
+            return ("stationary", "x", g, c)
+
+        def lt(g, h):
+            return ("stationary", "left", g, h)
+
+        ring = (4, 5, 6, 0, 1, 2, 3)
+
+        def multiply(g, n, j, step, first, last):
+            if first:
+                acc[g, n, j] = bank(j if n == 0 else ring[((2 * (n - 1) + g) * PACK + j) % len(ring)])
+            st, mv, c = passes[step]
+            if st == "x":
+                ks, q = xt(g, c), j
+            else:
+                ks, q = lt(g, j // 2), 2 * (j % 2) + c
+            km = moving(n, step)
+            cols = slice(q * P, (q + 1) * P)
+            nc.tensor.matmul_mx(
+                out=acc[g, n, j][:], lhsT=codes[ks][:, cols].bitcast(fmt(ks)), lhsT_scale=scales[ks][:, cols],
+                rhs=codes[km][:].bitcast(fmt(km)), rhs_scale=scales[km][:], start=first, stop=last)
+
+        def sweep(g, n, step, first=False, last=False):
+            for j in range(PACK):
+                multiply(g, n, j, step, first, last)
+
+        def gain(g, n, j):
+            scaled[g, n, j] = res.tile([P, S], F32, name="scaled")
+            nc.vector.scalar_tensor_tensor(
+                out=scaled[g, n, j][:], in0=acc[g, n, j][:], scalar=rg[:, g, j:j + 1], in1=rows[n][:, 0, :],
+                op0=ALU.mult, op1=ALU.mult)
+
+        def finish(g, n, j, engine=nc.vector):
+            t = scaled[g, n, j]
+            row = rows[n][:, 1, :] if n == 0 or engine is nc.gpsimd else psum_rows[:, (n - 1) * S:n * S]
+            engine.tensor_tensor(out=t[:], in0=t[:], in1=row, op=ALU.add)
+            dst = out[g * S:(g + 1) * S, n * S:(n + 1) * S].rearrange("(p j) w -> p j w", j=PACK)
+            nc.sync.dma_start(out=dst[:, j, :], in_=t[:])
+
+        load_left(0, 0, 1)
+        cols_in = keep.tile([P, 2, 16], BF16, name="cols_in")
+        for v, vec in enumerate((col_gain, background)):
+            nc.scalar.dma_start(out=cols_in[:, v, 0:12].rearrange("p (n e) -> p n e", e=PACK),
+                                in_=vec.rearrange("(n p e) -> p n e", p=P, e=PACK))
+        rg = keep.tile([P, 2, PACK], BF16, name="rg")
+        nc.scalar.dma_start(out=rg[:], in_=row_gain.rearrange("(g p j) -> p g j", p=P, j=PACK))
+        ident = keep.tile([P, P], F32, name="ident")
+        make_identity(nc, ident[:])
+
+        load("x", 0, 0, 1)
+        load_left(0, 1, 2)
+        load("right", 0, 0, 1)
+        load("x", 1, 0, 1)
+        load("x", 0, 1, 3)
+        load("right", 1, 0, 1)
+        load("right", 2, 0, 1)
+        load_left(1, 0, 2)
+        load("x", 1, 1, 3)
+        for n in (1, 2):
+            for c in range(3):
+                load("right", c, n, n + 1)
+        later_rows = keep.tile([P, 2, W - S], BF16, name="later_rows")
+        for v, vec in enumerate((col_gain, background)):
+            nc.sync.dma_start(out=later_rows[:, v, :], in_=vec[S:].partition_broadcast(P))
+
+        def warm(count):
+            return count
+
+        rows = []
+        col_words = cols_in[:].bitcast(F32)
+
+        def spread(n):
+            pt = bank(n)
+            for v in range(2):
+                for u in range(2):
+                    q = 2 * v + u
+                    w = 2 * n + u
+                    nc.tensor.transpose(pt[:, q * P:(q + 1) * P], col_words[:, v, w:w + 1].to_broadcast([P, P]), ident[:])
+            t = keep.tile([P, 2, S], BF16, name="rows%d" % n)
+            nc.scalar.copy(out=t[:].bitcast(F32).rearrange("p v (r u) -> p v r u", u=2),
+                           in_=pt[:].rearrange("p (v u r) -> p v r u", v=2, u=2))
+            rows.append(t)
+
+        A, B = (4, 5), (6, 7)
+        SH = 320
+        warm(0)
+        spread(0)
+        rows.extend(later_rows[:, :, (n - 1) * S:n * S] for n in (1, 2))
+        warm(0)
+        turn(lt(0, 0), A)
+        warm(0)
+        weave(moving(0, 0), S)
+        turn(xt(0, 0), B)
+        quantise(lt(0, 0))
+        turn(lt(0, 1), A)
+        quantise(moving(0, 0))
+        quantise(xt(0, 0))
+        weave(moving(0, 1), 256)
+        quantise(lt(0, 1))
+        sweep(0, 0, 0, first=True)
+        turn(xt(1, 0), B)
+        weave(moving(0, 2), S)
+        quantise(moving(0, 1))
+        sweep(0, 0, 1)
+        quantise(moving(0, 2))
+        turn(xt(0, 1), A)
+        turn(xt(0, 2), B)
+        weave(moving(0, 3), S)
+        sweep(0, 0, 2)
+        quantise(xt(1, 0))
+        quantise(xt(0, 1))
+        quantise(moving(0, 3))
+        weave(moving(0, 4), S)
+        sweep(0, 0, 3)
+        quantise(xt(0, 2))
+        quantise(moving(0, 4))
+        weave(moving(1, 0), 0)
+        sweep(0, 0, 4, last=True)
+        turn(lt(1, 0), A)
+        turn(lt(1, 1), B)
+        for j in range(PACK):
+            gain(0, 0, j)
+        finish(0, 0, 0, nc.gpsimd)
+        quantise(lt(1, 0))
+        quantise(lt(1, 1))
+        sweep(1, 0, 1, first=True)
+        weave(moving(1, 1), 0)
+        turn(xt(1, 1), A)
+        turn(xt(1, 2), B)
+        quantise(moving(1, 0))
+        weave(moving(1, 2), S)
+        sweep(1, 0, 0)
+        pt = bank(7)
+        for n in (1, 2):
+            for u in range(2):
+                nc.tensor.transpose(pt[:, (n - 1) * 2 * P + u:n * 2 * P:2], col_words[:, 1, 2 * n + u:2 * n + u + 1].to_broadcast([P, P]), ident[:])
+        psum_rows = pt[:].bitcast(BF16)
+        sweep(1, 0, 2)
+        quantise(moving(1, 1))
+        quantise(xt(1, 1))
+        quantise(xt(1, 2))
+        weave(moving(1, 3), 0)
+        quantise(moving(1, 2))
+
+        finish(0, 0, 1)
+        finish(0, 0, 2)
+        finish(0, 0, 3)
+        sweep(1, 0, 3)
+        sweep(1, 0, 4, last=True)
+        weave(moving(1, 4), 0)
+        quantise(moving(1, 3))
+        steps = len(passes)
+        other = nc.gpsimd
+        for j in range(PACK):
+            gain(1, 0, j)
+        finish(1, 0, 0, other)
+        quantise(moving(1, 4))
+        for step in range(steps):
+            sweep(0, 1, step, step == 0, step == steps - 1)
+        for j in range(1, PACK):
+            finish(1, 0, j)
+        for step in range(steps):
+            weave(moving(2, step), 0)
+        for j in range(PACK):
+            for step in range(steps):
+                multiply(1, 1, j, step, step == 0, step == steps - 1)
+        quantise(moving(2, 0))
+        for j in (0, 2):
+            gain(0, 1, j)
+            finish(0, 1, j, other)
+            gain(0, 1, j + 1)
+            finish(0, 1, j + 1)
+            quantise(moving(2, 1 + j // 2))
+        for j in (0, 2):
+            gain(1, 1, j)
+            finish(1, 1, j, other)
+            gain(1, 1, j + 1)
+            finish(1, 1, j + 1)
+            quantise(moving(2, 3 + j // 2))
+        for step in range(steps):
+            sweep(0, 2, step, step == 0, step == steps - 1)
+        for j in range(PACK):
+            for step in range(steps):
+                multiply(1, 2, j, step, step == 0, step == steps - 1)
+        for j in (0, 2):
+            gain(0, 2, j)
+            finish(0, 2, j, other)
+            gain(0, 2, j + 1)
+            finish(0, 2, j + 1)
+        for j in (0,):
+            gain(1, 2, j)
+            finish(1, 2, j, other)
+            gain(1, 2, j + 1)
+            finish(1, 2, j + 1)
+        gain(1, 2, 2)
+        finish(1, 2, 2)
+        gain(1, 2, 3)
+        finish(1, 2, 3)

@@ -120,6 +120,18 @@ def tile_additive_sylvester_transform_s2_kernel(tc, x, left, right, row_gain, co
                 out=scaled[g, n, j][:], in0=acc[g, n, j][:], scalar=rg[:, g, j:j + 1], in1=rows[n][:, 0, :],
                 op0=ALU.mult, op1=ALU.mult)
 
+        def last_tile(g, n, j):
+            dst = out[g * S:(g + 1) * S, n * S:(n + 1) * S].rearrange("(p j) w -> p j w", j=PACK)
+            halves = [res.tile([P, S // 2], F32, name="scaled") for _ in range(2)]
+            cols = [slice(h * S // 2, (h + 1) * S // 2) for h in range(2)]
+            for h in range(2):
+                nc.vector.scalar_tensor_tensor(
+                    out=halves[h][:], in0=acc[g, n, j][:, cols[h]], scalar=rg[:, g, j:j + 1], in1=rows[n][:, 0, cols[h]],
+                    op0=ALU.mult, op1=ALU.mult)
+            for h in range(2):
+                nc.vector.tensor_tensor(out=halves[h][:], in0=halves[h][:], in1=rows[n][:, 1, cols[h]], op=ALU.add)
+                nc.sync.dma_start(out=dst[:, j, cols[h]], in_=halves[h][:])
+
         def finish(g, n, j, engine=nc.vector):
             t = scaled[g, n, j]
             row = rows[n][:, 1, :] if n == 0 or engine is nc.gpsimd else psum_rows[:, (n - 1) * S:n * S]
@@ -141,10 +153,12 @@ def tile_additive_sylvester_transform_s2_kernel(tc, x, left, right, row_gain, co
         load_left(0, 1, 2)
         load("right", 0, 0, 1)
         load("x", 1, 0, 1)
-        load("x", 0, 1, 3)
+        load("x", 0, 1, 2)
         load("right", 1, 0, 1)
+        load("x", 0, 2, 3)
         load("right", 2, 0, 1)
-        load_left(1, 0, 2)
+        load_left(1, 0, 1)
+        load_left(1, 1, 2)
         load("x", 1, 1, 3)
         for n in (1, 2):
             for c in range(3):
@@ -153,8 +167,17 @@ def tile_additive_sylvester_transform_s2_kernel(tc, x, left, right, row_gain, co
         for v, vec in enumerate((col_gain, background)):
             nc.sync.dma_start(out=later_rows[:, v, :], in_=vec[S:].partition_broadcast(P))
 
+        blank = keep.tile([P, PACK * S], BF16, name="blank", align_bytes=64)
+        nc.vector.memset(blank[:], 0.0)
+        grouped["moving", "blank", 0, 0] = blank
+        quantise(("moving", "blank", 0, 0))
+        wc, ws = codes["moving", "blank", 0, 0], scales["moving", "blank", 0, 0]
+
         def warm(count):
-            return count
+            idle = bank(3)
+            for _ in range(count):
+                nc.tensor.matmul_mx(out=idle[:], lhsT=wc[:, :P].bitcast(E4M3), lhsT_scale=ws[:, :P],
+                                    rhs=wc[:].bitcast(E4M3), rhs_scale=ws[:], start=True, stop=True)
 
         rows = []
         col_words = cols_in[:].bitcast(F32)
@@ -173,40 +196,49 @@ def tile_additive_sylvester_transform_s2_kernel(tc, x, left, right, row_gain, co
 
         A, B = (4, 5), (6, 7)
         SH = 320
-        warm(0)
+        warm(5)
         spread(0)
         rows.extend(later_rows[:, :, (n - 1) * S:n * S] for n in (1, 2))
-        warm(0)
+        warm(1)
+        steps = len(passes)
+
+        def tile_major(g, n, j):
+            for step in range(steps):
+                multiply(g, n, j, step, step == 0, step == steps - 1)
+
         turn(lt(0, 0), A)
-        warm(0)
+        warm(1)
         weave(moving(0, 0), S)
         turn(xt(0, 0), B)
         quantise(lt(0, 0))
         turn(lt(0, 1), A)
         quantise(moving(0, 0))
-        quantise(xt(0, 0))
-        weave(moving(0, 1), 256)
+        warm(1)
+        weave(moving(0, 1), 128)
         quantise(lt(0, 1))
+        quantise(xt(0, 0))
         sweep(0, 0, 0, first=True)
         turn(xt(1, 0), B)
-        weave(moving(0, 2), S)
+        weave(moving(0, 2), 320)
         quantise(moving(0, 1))
         sweep(0, 0, 1)
-        quantise(moving(0, 2))
         turn(xt(0, 1), A)
-        turn(xt(0, 2), B)
-        weave(moving(0, 3), S)
+
+        weave(moving(0, 3), 320)
+        quantise(moving(0, 2))
         sweep(0, 0, 2)
-        quantise(xt(1, 0))
         quantise(xt(0, 1))
+        quantise(xt(1, 0))
+        turn(xt(0, 2), B)
         quantise(moving(0, 3))
-        weave(moving(0, 4), S)
+        weave(moving(0, 4), 416)
         sweep(0, 0, 3)
         quantise(xt(0, 2))
         quantise(moving(0, 4))
         weave(moving(1, 0), 0)
-        sweep(0, 0, 4, last=True)
         turn(lt(1, 0), A)
+        sweep(0, 0, 4, last=True)
+
         turn(lt(1, 1), B)
         for j in range(PACK):
             gain(0, 0, j)
@@ -214,75 +246,72 @@ def tile_additive_sylvester_transform_s2_kernel(tc, x, left, right, row_gain, co
         quantise(lt(1, 0))
         quantise(lt(1, 1))
         sweep(1, 0, 1, first=True)
-        weave(moving(1, 1), 0)
-        turn(xt(1, 1), A)
-        turn(xt(1, 2), B)
-        quantise(moving(1, 0))
-        weave(moving(1, 2), S)
-        sweep(1, 0, 0)
+
         pt = bank(7)
         for n in (1, 2):
             for u in range(2):
                 nc.tensor.transpose(pt[:, (n - 1) * 2 * P + u:n * 2 * P:2], col_words[:, 1, 2 * n + u:2 * n + u + 1].to_broadcast([P, P]), ident[:])
         psum_rows = pt[:].bitcast(BF16)
+        turn(xt(1, 1), A)
+        turn(xt(1, 2), (6, 4))
+        weave(moving(1, 1), 256)
+        quantise(moving(1, 0))
+        weave(moving(1, 2), S)
+        sweep(1, 0, 0)
         sweep(1, 0, 2)
-        quantise(moving(1, 1))
         quantise(xt(1, 1))
         quantise(xt(1, 2))
+        finish(0, 0, 1)
+        quantise(moving(1, 1))
         weave(moving(1, 3), 0)
         quantise(moving(1, 2))
-
-        finish(0, 0, 1)
         finish(0, 0, 2)
         finish(0, 0, 3)
         sweep(1, 0, 3)
         sweep(1, 0, 4, last=True)
         weave(moving(1, 4), 0)
-        quantise(moving(1, 3))
-        steps = len(passes)
-        other = nc.gpsimd
         for j in range(PACK):
             gain(1, 0, j)
-        finish(1, 0, 0, other)
+        finish(1, 0, 0, nc.gpsimd)
+        quantise(moving(1, 3))
+        finish(1, 0, 1)
         quantise(moving(1, 4))
         for step in range(steps):
             sweep(0, 1, step, step == 0, step == steps - 1)
-        for j in range(1, PACK):
-            finish(1, 0, j)
+        finish(1, 0, 2)
         for step in range(steps):
             weave(moving(2, step), 0)
-        for j in range(PACK):
-            for step in range(steps):
-                multiply(1, 1, j, step, step == 0, step == steps - 1)
+        def pair(g, n, j, earlier):
+            gain(g, n, j)
+            finish(g, n, j, nc.gpsimd)
+            gain(g, n, j + 1)
+            finish(*earlier)
+
         quantise(moving(2, 0))
-        for j in (0, 2):
-            gain(0, 1, j)
-            finish(0, 1, j, other)
-            gain(0, 1, j + 1)
-            finish(0, 1, j + 1)
-            quantise(moving(2, 1 + j // 2))
-        for j in (0, 2):
-            gain(1, 1, j)
-            finish(1, 1, j, other)
-            gain(1, 1, j + 1)
-            finish(1, 1, j + 1)
-            quantise(moving(2, 3 + j // 2))
+        pair(0, 1, 0, (1, 0, 3))
+        quantise(moving(2, 1))
+        pair(0, 1, 2, (0, 1, 1))
+        quantise(moving(2, 2))
+        for j in range(PACK):
+            tile_major(1, 1, j)
+        pair(1, 1, 0, (0, 1, 3))
+        quantise(moving(2, 3))
+        pair(1, 1, 2, (1, 1, 1))
+        quantise(moving(2, 4))
+        finish(1, 1, 3)
         for step in range(steps):
             sweep(0, 2, step, step == 0, step == steps - 1)
+        gain(0, 2, 0)
+        finish(0, 2, 0, nc.gpsimd)
+        gain(0, 2, 1)
+        gain(0, 2, 2)
+        finish(0, 2, 2, nc.gpsimd)
+        gain(0, 2, 3)
+        finish(0, 2, 1)
         for j in range(PACK):
-            for step in range(steps):
-                multiply(1, 2, j, step, step == 0, step == steps - 1)
-        for j in (0, 2):
-            gain(0, 2, j)
-            finish(0, 2, j, other)
-            gain(0, 2, j + 1)
-            finish(0, 2, j + 1)
-        for j in (0,):
-            gain(1, 2, j)
-            finish(1, 2, j, other)
-            gain(1, 2, j + 1)
-            finish(1, 2, j + 1)
+            tile_major(1, 2, j)
+        pair(1, 2, 0, (0, 2, 3))
         gain(1, 2, 2)
+        finish(1, 2, 1)
         finish(1, 2, 2)
-        gain(1, 2, 3)
-        finish(1, 2, 3)
+        last_tile(1, 2, 3)

@@ -18,20 +18,32 @@ P = 128
 PACK = 4
 S = P * PACK
 
+PASSES = (("left", "x", 0), ("x", "right", 0), ("left", "x", 1), ("x", "right", 1), ("x", "right", 2))
+STEPS = len(PASSES)
+
 
 def tile_additive_sylvester_transform_s2_kernel(tc, x, left, right, row_gain, col_gain, background, out):
     nc = tc.nc
     with ExitStack() as ctx:
         keep = ctx.enter_context(tc.tile_pool(name="keep", bufs=1))
-        stage = ctx.enter_context(tc.tile_pool(name="stage", bufs=8))
+        stage = ctx.enter_context(tc.tile_pool(name="stage", bufs=9))
         res = ctx.enter_context(tc.tile_pool(name="res", bufs=12))
         psum = ctx.enter_context(tc.psum_pool(name="psum", bufs=1))
         ctx.enter_context(tc.manual_schedule())
 
-        raw, grouped, codes, scales = {}, {}, {}, {}
+        raw, parted, grouped, codes, scales, acc, scaled = {}, {}, {}, {}, {}, {}, {}
 
         def bank(b):
             return psum.tile([P, S], F32, name="bank%d" % b)
+
+        def moving(n, step):
+            return ("moving", PASSES[step][1], PASSES[step][2], n)
+
+        def xt(g, c):
+            return ("stationary", "x", g, c)
+
+        def lt(g, h):
+            return ("stationary", "left", g, h)
 
         def load(which, r, c0, c1):
             src = x if which == "x" else right
@@ -40,11 +52,10 @@ def tile_additive_sylvester_transform_s2_kernel(tc, x, left, right, row_gain, co
             for c in range(c0, c1):
                 raw[which, r, c] = t[:, :, (c - c0) * S:(c - c0 + 1) * S]
 
-        def load_left(g, h0, h1):
-            t = keep.tile([P, 2 * (h1 - h0), H], BF16, name="raw_left%d%d" % (g, h0), align_bytes=64)
-            nc.sync.dma_start(out=t[:], in_=left[g * S:(g + 1) * S, :].rearrange("(p j) w -> p j w", j=PACK)[:, 2 * h0:2 * h1, :])
-            for h in range(h0, h1):
-                raw["left", g, h] = t[:, 2 * (h - h0):2 * (h - h0 + 1), :].rearrange("p j (c w) -> p (j c) w", c=2)
+        def load_left(g, h):
+            t = keep.tile([P, 2, H], BF16, name="raw_left%d%d" % (g, h), align_bytes=64)
+            nc.sync.dma_start(out=t[:], in_=left[g * S:(g + 1) * S, :].rearrange("(p j) w -> p j w", j=PACK)[:, 2 * h:2 * h + 2, :])
+            raw["left", g, h] = t[:].rearrange("p j (c w) -> p (j c) w", c=2)
 
         def weave(key, on_vector):
             g = stage.tile([P, PACK * S], BF16, name="grouped", align_bytes=64)
@@ -57,6 +68,12 @@ def tile_additive_sylvester_transform_s2_kernel(tc, x, left, right, row_gain, co
                 nc.scalar.copy(out=dst[:, cut:], in_=src[:, cut:])
             grouped[key] = g
 
+        def part(key):
+            t = stage.tile([P, PACK, 2, P], F32, name="parted", bufs=3, align_bytes=64)
+            nc.vector.tensor_copy(out=t[:].rearrange("p j u (b m) -> p j b u m", m=4),
+                                  in_=raw[key[1:]].bitcast(F32).rearrange("p j (b m u) -> p j b u m", m=4, u=2))
+            parted[key] = t
+
         def turn(key, banks):
             g = stage.tile([P, PACK * S], BF16, name="grouped", align_bytes=64)
             words = raw[key[1:]].bitcast(F32)
@@ -64,9 +81,11 @@ def tile_additive_sylvester_transform_s2_kernel(tc, x, left, right, row_gain, co
             for half in range(2):
                 pt = bank(banks[half])
                 for jj in range(2):
+                    j = 2 * half + jj
                     for u in range(2):
                         q = 2 * jj + u
-                        nc.tensor.transpose(pt[:, q * P:(q + 1) * P], words[:, 2 * half + jj, u:2 * P:2], ident[:])
+                        src = parted[key][:, j, u, :] if key in parted else words[:, j, u:2 * P:2]
+                        nc.tensor.transpose(pt[:, q * P:(q + 1) * P], src, ident[:])
                 nc.scalar.copy(
                     out=g_words[:, half * S:(half + 1) * S].rearrange("p (j r u) -> p j r u", j=2, u=2),
                     in_=pt[:].rearrange("p (j u r) -> p j r u", j=2, u=2),
@@ -82,28 +101,13 @@ def tile_additive_sylvester_transform_s2_kernel(tc, x, left, right, row_gain, co
             scales[key] = keep.tile([P, S], U8, name="s_" + name, align_bytes=64)
             nc.vector.quantize_mx(out=codes[key][:].bitcast(fmt(key)), scales=scales[key][:], in_=grouped[key][:])
 
-        passes = [("left", "x", 0), ("x", "right", 0), ("left", "x", 1), ("x", "right", 1), ("x", "right", 2)]
-        acc, scaled = {}, {}
-
-        def moving(n, step):
-            return ("moving", passes[step][1], passes[step][2], n)
-
-        def xt(g, c):
-            return ("stationary", "x", g, c)
-
-        def lt(g, h):
-            return ("stationary", "left", g, h)
-
         ring = (4, 5, 6, 0, 1, 2, 3)
 
         def multiply(g, n, j, step, first, last):
             if first:
                 acc[g, n, j] = bank(j if n == 0 else ring[((2 * (n - 1) + g) * PACK + j) % len(ring)])
-            st, mv, c = passes[step]
-            if st == "x":
-                ks, q = xt(g, c), j
-            else:
-                ks, q = lt(g, j // 2), 2 * (j % 2) + c
+            st, _, c = PASSES[step]
+            ks, q = (xt(g, c), j) if st == "x" else (lt(g, j // 2), 2 * (j % 2) + c)
             km = moving(n, step)
             cols = slice(q * P, (q + 1) * P)
             nc.tensor.matmul_mx(
@@ -114,32 +118,39 @@ def tile_additive_sylvester_transform_s2_kernel(tc, x, left, right, row_gain, co
             for j in range(PACK):
                 multiply(g, n, j, step, first, last)
 
-        def gain(g, n, j):
-            scaled[g, n, j] = res.tile([P, S], F32, name="scaled")
+        def pass_by_pass(g, n):
+            for step in range(STEPS):
+                sweep(g, n, step, step == 0, step == STEPS - 1)
+
+        def tile_by_tile(g, n):
+            for j in range(PACK):
+                for step in range(STEPS):
+                    multiply(g, n, j, step, step == 0, step == STEPS - 1)
+
+        def gain(g, n, j, cols=slice(0, S)):
+            t = res.tile([P, cols.stop - cols.start], F32, name="scaled")
             nc.vector.scalar_tensor_tensor(
-                out=scaled[g, n, j][:], in0=acc[g, n, j][:], scalar=rg[:, g, j:j + 1], in1=rows[n][:, 0, :],
+                out=t[:], in0=acc[g, n, j][:, cols], scalar=rg[:, g, j:j + 1], in1=rows[n][:, 0, cols],
                 op0=ALU.mult, op1=ALU.mult)
+            scaled[g, n, j, cols.start] = t
 
-        def last_tile(g, n, j):
-            dst = out[g * S:(g + 1) * S, n * S:(n + 1) * S].rearrange("(p j) w -> p j w", j=PACK)
-            halves = [res.tile([P, S // 2], F32, name="scaled") for _ in range(2)]
-            cols = [slice(h * S // 2, (h + 1) * S // 2) for h in range(2)]
-            for h in range(2):
-                nc.vector.scalar_tensor_tensor(
-                    out=halves[h][:], in0=acc[g, n, j][:, cols[h]], scalar=rg[:, g, j:j + 1], in1=rows[n][:, 0, cols[h]],
-                    op0=ALU.mult, op1=ALU.mult)
-            for h in range(2):
-                nc.vector.tensor_tensor(out=halves[h][:], in0=halves[h][:], in1=rows[n][:, 1, cols[h]], op=ALU.add)
-                nc.sync.dma_start(out=dst[:, j, cols[h]], in_=halves[h][:])
-
-        def finish(g, n, j, engine=nc.vector):
-            t = scaled[g, n, j]
+        def finish(g, n, j, engine=nc.vector, cols=slice(0, S)):
+            t = scaled[g, n, j, cols.start]
             row = rows[n][:, 1, :] if n == 0 or engine is nc.gpsimd else psum_rows[:, (n - 1) * S:n * S]
-            engine.tensor_tensor(out=t[:], in0=t[:], in1=row, op=ALU.add)
+            engine.tensor_tensor(out=t[:], in0=t[:], in1=row[:, cols], op=ALU.add)
             dst = out[g * S:(g + 1) * S, n * S:(n + 1) * S].rearrange("(p j) w -> p j w", j=PACK)
-            nc.sync.dma_start(out=dst[:, j, :], in_=t[:])
+            nc.sync.dma_start(out=dst[:, j, cols], in_=t[:])
 
-        load_left(0, 0, 1)
+        def drain(g, n):
+            for j in range(PACK):
+                gain(g, n, j)
+                if j == 0 or (j == 2 and n > 0):
+                    finish(g, n, j, nc.gpsimd)
+            if n > 0:
+                finish(g, n, 1)
+                finish(g, n, 3)
+
+        load_left(0, 0)
         cols_in = keep.tile([P, 2, 16], BF16, name="cols_in")
         for v, vec in enumerate((col_gain, background)):
             nc.scalar.dma_start(out=cols_in[:, v, 0:12].rearrange("p (n e) -> p n e", e=PACK),
@@ -148,170 +159,129 @@ def tile_additive_sylvester_transform_s2_kernel(tc, x, left, right, row_gain, co
         nc.scalar.dma_start(out=rg[:], in_=row_gain.rearrange("(g p j) -> p g j", p=P, j=PACK))
         ident = keep.tile([P, P], F32, name="ident")
         make_identity(nc, ident[:])
-
         load("x", 0, 0, 1)
-        load_left(0, 1, 2)
+        load_left(0, 1)
         load("right", 0, 0, 1)
         load("x", 1, 0, 1)
         load("x", 0, 1, 2)
         load("right", 1, 0, 1)
         load("x", 0, 2, 3)
         load("right", 2, 0, 1)
-        load_left(1, 0, 1)
-        load_left(1, 1, 2)
+        load_left(1, 0)
+        load_left(1, 1)
         load("x", 1, 1, 3)
         for n in (1, 2):
             for c in range(3):
                 load("right", c, n, n + 1)
-        later_rows = keep.tile([P, 2, W - S], BF16, name="later_rows")
-        for v, vec in enumerate((col_gain, background)):
-            nc.sync.dma_start(out=later_rows[:, v, :], in_=vec[S:].partition_broadcast(P))
 
-        blank = keep.tile([P, PACK * S], BF16, name="blank", align_bytes=64)
-        nc.vector.memset(blank[:], 0.0)
-        grouped["moving", "blank", 0, 0] = blank
-        quantise(("moving", "blank", 0, 0))
-        wc, ws = codes["moving", "blank", 0, 0], scales["moving", "blank", 0, 0]
-
-        def warm(count):
-            idle = bank(3)
-            for _ in range(count):
-                nc.tensor.matmul_mx(out=idle[:], lhsT=wc[:, :P].bitcast(E4M3), lhsT_scale=ws[:, :P],
-                                    rhs=wc[:].bitcast(E4M3), rhs_scale=ws[:], start=True, stop=True)
-
-        rows = []
         col_words = cols_in[:].bitcast(F32)
+
+        def column(v, n, u):
+            return col_words[:, v, 2 * n + u:2 * n + u + 1].to_broadcast([P, P])
 
         def spread(n):
             pt = bank(n)
             for v in range(2):
                 for u in range(2):
-                    q = 2 * v + u
-                    w = 2 * n + u
-                    nc.tensor.transpose(pt[:, q * P:(q + 1) * P], col_words[:, v, w:w + 1].to_broadcast([P, P]), ident[:])
+                    nc.tensor.transpose(pt[:, (2 * v + u) * P:(2 * v + u + 1) * P], column(v, n, u), ident[:])
             t = keep.tile([P, 2, S], BF16, name="rows%d" % n)
             nc.scalar.copy(out=t[:].bitcast(F32).rearrange("p v (r u) -> p v r u", u=2),
                            in_=pt[:].rearrange("p (v u r) -> p v r u", v=2, u=2))
-            rows.append(t)
+            return t
+
+        rows = [spread(0)]
 
         A, B = (4, 5), (6, 7)
-        SH = 320
-        warm(5)
-        spread(0)
-        rows.extend(later_rows[:, :, (n - 1) * S:n * S] for n in (1, 2))
-        warm(1)
-        steps = len(passes)
-
-        def tile_major(g, n, j):
-            for step in range(steps):
-                multiply(g, n, j, step, step == 0, step == steps - 1)
-
         turn(lt(0, 0), A)
-        warm(1)
+        rows.append(spread(1))
         weave(moving(0, 0), S)
         turn(xt(0, 0), B)
         quantise(lt(0, 0))
         turn(lt(0, 1), A)
+        rows.append(spread(2))
         quantise(moving(0, 0))
-        warm(1)
         weave(moving(0, 1), 128)
         quantise(lt(0, 1))
         quantise(xt(0, 0))
         sweep(0, 0, 0, first=True)
         turn(xt(1, 0), B)
-        weave(moving(0, 2), 320)
+        weave(moving(0, 2), S)
         quantise(moving(0, 1))
         sweep(0, 0, 1)
         turn(xt(0, 1), A)
-
-        weave(moving(0, 3), 320)
         quantise(moving(0, 2))
+        weave(moving(0, 3), S)
         sweep(0, 0, 2)
+        weave(moving(1, 0), 256)
         quantise(xt(0, 1))
-        quantise(xt(1, 0))
         turn(xt(0, 2), B)
         quantise(moving(0, 3))
         weave(moving(0, 4), 416)
         sweep(0, 0, 3)
         quantise(xt(0, 2))
         quantise(moving(0, 4))
-        weave(moving(1, 0), 0)
+        weave(moving(2, 0), 0)
         turn(lt(1, 0), A)
+        quantise(xt(1, 0))
+        quantise(moving(1, 0))
         sweep(0, 0, 4, last=True)
-
         turn(lt(1, 1), B)
-        for j in range(PACK):
-            gain(0, 0, j)
-        finish(0, 0, 0, nc.gpsimd)
+        drain(0, 0)
+        part(xt(1, 1))
+        part(xt(1, 2))
         quantise(lt(1, 0))
         quantise(lt(1, 1))
         sweep(1, 0, 1, first=True)
-
         pt = bank(7)
         for n in (1, 2):
             for u in range(2):
-                nc.tensor.transpose(pt[:, (n - 1) * 2 * P + u:n * 2 * P:2], col_words[:, 1, 2 * n + u:2 * n + u + 1].to_broadcast([P, P]), ident[:])
+                nc.tensor.transpose(pt[:, (n - 1) * 2 * P + u:n * 2 * P:2], column(1, n, u), ident[:])
         psum_rows = pt[:].bitcast(BF16)
         turn(xt(1, 1), A)
         turn(xt(1, 2), (6, 4))
-        weave(moving(1, 1), 256)
-        quantise(moving(1, 0))
         weave(moving(1, 2), S)
-        sweep(1, 0, 0)
-        sweep(1, 0, 2)
         quantise(xt(1, 1))
         quantise(xt(1, 2))
-        finish(0, 0, 1)
-        quantise(moving(1, 1))
-        weave(moving(1, 3), 0)
+        weave(moving(1, 1), 256)
+        sweep(1, 0, 0)
+        sweep(1, 0, 2)
+        quantise(moving(2, 0))
         quantise(moving(1, 2))
-        finish(0, 0, 2)
-        finish(0, 0, 3)
+        quantise(moving(1, 1))
         sweep(1, 0, 3)
         sweep(1, 0, 4, last=True)
-        weave(moving(1, 4), 0)
-        for j in range(PACK):
-            gain(1, 0, j)
-        finish(1, 0, 0, nc.gpsimd)
+        for n, step in ((1, 3), (1, 4), (2, 1), (2, 2)):
+            weave(moving(n, step), 0)
+        drain(1, 0)
         quantise(moving(1, 3))
-        finish(1, 0, 1)
+        finish(0, 0, 1)
         quantise(moving(1, 4))
-        for step in range(steps):
-            sweep(0, 1, step, step == 0, step == steps - 1)
+        pass_by_pass(0, 1)
+        finish(0, 0, 2)
+        finish(0, 0, 3)
+        finish(1, 0, 1)
         finish(1, 0, 2)
-        for step in range(steps):
+        drain(0, 1)
+        for step in (3, 4):
             weave(moving(2, step), 0)
-        def pair(g, n, j, earlier):
-            gain(g, n, j)
-            finish(g, n, j, nc.gpsimd)
-            gain(g, n, j + 1)
-            finish(*earlier)
-
-        quantise(moving(2, 0))
-        pair(0, 1, 0, (1, 0, 3))
         quantise(moving(2, 1))
-        pair(0, 1, 2, (0, 1, 1))
         quantise(moving(2, 2))
-        for j in range(PACK):
-            tile_major(1, 1, j)
-        pair(1, 1, 0, (0, 1, 3))
+        finish(1, 0, 3)
+        tile_by_tile(1, 1)
+        drain(1, 1)
         quantise(moving(2, 3))
-        pair(1, 1, 2, (1, 1, 1))
         quantise(moving(2, 4))
-        finish(1, 1, 3)
-        for step in range(steps):
-            sweep(0, 2, step, step == 0, step == steps - 1)
-        gain(0, 2, 0)
-        finish(0, 2, 0, nc.gpsimd)
-        gain(0, 2, 1)
-        gain(0, 2, 2)
-        finish(0, 2, 2, nc.gpsimd)
-        gain(0, 2, 3)
-        finish(0, 2, 1)
-        for j in range(PACK):
-            tile_major(1, 2, j)
-        pair(1, 2, 0, (0, 2, 3))
-        gain(1, 2, 2)
+        pass_by_pass(0, 2)
+        drain(0, 2)
+        tile_by_tile(1, 2)
+        gain(1, 2, 0)
+        finish(1, 2, 0, nc.gpsimd)
+        gain(1, 2, 1)
         finish(1, 2, 1)
+        gain(1, 2, 2)
         finish(1, 2, 2)
-        last_tile(1, 2, 3)
+        halves = (slice(0, S // 2), slice(S // 2, S))
+        for cols in halves:
+            gain(1, 2, 3, cols)
+        for cols in halves:
+            finish(1, 2, 3, cols=cols)

@@ -27,7 +27,7 @@ def tile_additive_sylvester_transform_s2_kernel(tc, x, left, right, row_gain, co
     with ExitStack() as ctx:
         keep = ctx.enter_context(tc.tile_pool(name="keep", bufs=1))
         stage = ctx.enter_context(tc.tile_pool(name="stage", bufs=9))
-        res = ctx.enter_context(tc.tile_pool(name="res", bufs=12))
+        res = ctx.enter_context(tc.tile_pool(name="res", bufs=14))
         psum = ctx.enter_context(tc.psum_pool(name="psum", bufs=1))
         ctx.enter_context(tc.manual_schedule())
 
@@ -57,16 +57,12 @@ def tile_additive_sylvester_transform_s2_kernel(tc, x, left, right, row_gain, co
             nc.sync.dma_start(out=t[:], in_=left[g * S:(g + 1) * S, :].rearrange("(p j) w -> p j w", j=PACK)[:, 2 * h:2 * h + 2, :])
             raw["left", g, h] = t[:].rearrange("p j (c w) -> p (j c) w", c=2)
 
-        def weave(key, on_vector):
-            g = stage.tile([P, PACK * S], BF16, name="grouped", align_bytes=64)
-            dst = g[:].rearrange("p (c i t) -> p c t i", i=4, t=PACK)
+        def weave(key, copy, lo=0, hi=S):
+            if key not in grouped:
+                grouped[key] = stage.tile([P, PACK * S], BF16, name="grouped", align_bytes=64)
+            dst = grouped[key][:].rearrange("p (c i t) -> p c t i", i=4, t=PACK)
             src = raw[key[1:]].rearrange("p t (c i) -> p c t i", i=4)
-            cut = on_vector // 4
-            if on_vector > 0:
-                nc.vector.tensor_copy(out=dst[:, :cut], in_=src[:, :cut])
-            if on_vector < S:
-                nc.scalar.copy(out=dst[:, cut:], in_=src[:, cut:])
-            grouped[key] = g
+            copy(out=dst[:, lo // 4:hi // 4], in_=src[:, lo // 4:hi // 4])
 
         def part(key):
             t = stage.tile([P, PACK, 2, P], F32, name="parted", bufs=3, align_bytes=64)
@@ -192,40 +188,47 @@ def tile_additive_sylvester_transform_s2_kernel(tc, x, left, right, row_gain, co
         rows = [spread(0)]
 
         A, B = (4, 5), (6, 7)
+        vector, scalar = nc.vector.tensor_copy, nc.scalar.copy
         turn(lt(0, 0), A)
         rows.append(spread(1))
-        weave(moving(0, 0), S)
+        weave(moving(0, 0), vector)
         turn(xt(0, 0), B)
         quantise(lt(0, 0))
         turn(lt(0, 1), A)
         rows.append(spread(2))
         quantise(moving(0, 0))
-        weave(moving(0, 1), 128)
+        weave(moving(0, 1), vector, 0, 128)
+        weave(moving(0, 1), scalar, 128, S)
         quantise(lt(0, 1))
         quantise(xt(0, 0))
         sweep(0, 0, 0, first=True)
         turn(xt(1, 0), B)
-        weave(moving(0, 2), S)
+        weave(moving(0, 2), vector)
         quantise(moving(0, 1))
         sweep(0, 0, 1)
+        weave(moving(1, 0), scalar, 0, S // 2)
         turn(xt(0, 1), A)
         quantise(moving(0, 2))
-        weave(moving(0, 3), S)
+        weave(moving(0, 3), vector)
         sweep(0, 0, 2)
-        weave(moving(1, 0), 256)
+        weave(moving(1, 0), scalar, S // 2, S)
+        quantise(xt(1, 0))
+        weave(moving(2, 0), vector, 0, 320)
         quantise(xt(0, 1))
         turn(xt(0, 2), B)
         quantise(moving(0, 3))
-        weave(moving(0, 4), 416)
+        weave(moving(0, 4), vector, 0, 416)
+        weave(moving(0, 4), scalar, 416, S)
         sweep(0, 0, 3)
         quantise(xt(0, 2))
         quantise(moving(0, 4))
-        weave(moving(2, 0), 0)
-        turn(lt(1, 0), A)
-        quantise(xt(1, 0))
         quantise(moving(1, 0))
+        turn(lt(1, 0), A)
+        weave(moving(2, 0), vector, 320, S)
+        weave(moving(1, 2), scalar, 0, S // 2)
         sweep(0, 0, 4, last=True)
         turn(lt(1, 1), B)
+        weave(moving(1, 2), scalar, S // 2, S)
         drain(0, 0)
         part(xt(1, 1))
         part(xt(1, 2))
@@ -239,10 +242,10 @@ def tile_additive_sylvester_transform_s2_kernel(tc, x, left, right, row_gain, co
         psum_rows = pt[:].bitcast(BF16)
         turn(xt(1, 1), A)
         turn(xt(1, 2), (6, 4))
-        weave(moving(1, 2), S)
+        weave(moving(1, 1), vector, 0, 256)
+        weave(moving(1, 1), scalar, 256, S)
         quantise(xt(1, 1))
         quantise(xt(1, 2))
-        weave(moving(1, 1), 256)
         sweep(1, 0, 0)
         sweep(1, 0, 2)
         quantise(moving(2, 0))
@@ -251,33 +254,32 @@ def tile_additive_sylvester_transform_s2_kernel(tc, x, left, right, row_gain, co
         sweep(1, 0, 3)
         sweep(1, 0, 4, last=True)
         for n, step in ((1, 3), (1, 4), (2, 1), (2, 2)):
-            weave(moving(n, step), 0)
+            weave(moving(n, step), scalar)
         drain(1, 0)
         quantise(moving(1, 3))
         finish(0, 0, 1)
+        finish(0, 0, 2)
         quantise(moving(1, 4))
         pass_by_pass(0, 1)
-        finish(0, 0, 2)
         finish(0, 0, 3)
         finish(1, 0, 1)
-        finish(1, 0, 2)
         drain(0, 1)
         for step in (3, 4):
-            weave(moving(2, step), 0)
+            weave(moving(2, step), scalar)
         quantise(moving(2, 1))
         quantise(moving(2, 2))
-        finish(1, 0, 3)
         tile_by_tile(1, 1)
         drain(1, 1)
         quantise(moving(2, 3))
         quantise(moving(2, 4))
+        finish(1, 0, 2)
+        finish(1, 0, 3)
         pass_by_pass(0, 2)
         drain(0, 2)
         tile_by_tile(1, 2)
-        gain(1, 2, 0)
-        finish(1, 2, 0, nc.gpsimd)
-        gain(1, 2, 1)
-        finish(1, 2, 1)
+        for j in range(2):
+            gain(1, 2, j)
+            finish(1, 2, j, nc.gpsimd)
         gain(1, 2, 2)
         finish(1, 2, 2)
         halves = (slice(0, S // 2), slice(S // 2, S))

@@ -17,21 +17,36 @@ ALU = mybir.AluOpType
 P = 128
 PACK = 4
 S = P * PACK
+HALF = S // 2
+RUN = 4
 
 PASSES = (("left", "x", 0), ("x", "right", 0), ("left", "x", 1), ("x", "right", 1), ("x", "right", 2))
 STEPS = len(PASSES)
+
+PAIR_A, PAIR_B = (4, 5), (6, 7)
+PAIR_LAST = (6, 4)
+BACKGROUND_BANK = 7
+RING = (4, 5, 6, 0, 1, 2, 3)
+
+STAGE_BUFS = 9
+PARTED_BUFS = 2
+RESULT_BUFS = 14
+
+VECTOR_SHARE_RIGHT00 = 128
+VECTOR_SHARE_X02 = 320
 
 
 def tile_additive_sylvester_transform_s2_kernel(tc, x, left, right, row_gain, col_gain, background, out):
     nc = tc.nc
     with ExitStack() as ctx:
         keep = ctx.enter_context(tc.tile_pool(name="keep", bufs=1))
-        stage = ctx.enter_context(tc.tile_pool(name="stage", bufs=9))
-        res = ctx.enter_context(tc.tile_pool(name="res", bufs=14))
+        stage = ctx.enter_context(tc.tile_pool(name="stage", bufs=STAGE_BUFS))
+        res = ctx.enter_context(tc.tile_pool(name="res", bufs=RESULT_BUFS))
         psum = ctx.enter_context(tc.psum_pool(name="psum", bufs=1))
         ctx.enter_context(tc.manual_schedule())
 
         raw, parted, grouped, codes, scales, acc, scaled = {}, {}, {}, {}, {}, {}, {}
+        vector, scalar = nc.vector.tensor_copy, nc.scalar.copy
 
         def bank(b):
             return psum.tile([P, S], F32, name="bank%d" % b)
@@ -60,14 +75,14 @@ def tile_additive_sylvester_transform_s2_kernel(tc, x, left, right, row_gain, co
         def weave(key, copy, lo=0, hi=S):
             if key not in grouped:
                 grouped[key] = stage.tile([P, PACK * S], BF16, name="grouped", align_bytes=64)
-            dst = grouped[key][:].rearrange("p (c i t) -> p c t i", i=4, t=PACK)
-            src = raw[key[1:]].rearrange("p t (c i) -> p c t i", i=4)
-            copy(out=dst[:, lo // 4:hi // 4], in_=src[:, lo // 4:hi // 4])
+            dst = grouped[key][:].rearrange("p (c i t) -> p c t i", i=RUN, t=PACK)
+            src = raw[key[1:]].rearrange("p t (c i) -> p c t i", i=RUN)
+            copy(out=dst[:, lo // RUN:hi // RUN], in_=src[:, lo // RUN:hi // RUN])
 
         def part(key):
-            t = stage.tile([P, PACK, 2, P], F32, name="parted", bufs=3, align_bytes=64)
-            nc.vector.tensor_copy(out=t[:].rearrange("p j u (b m) -> p j b u m", m=4),
-                                  in_=raw[key[1:]].bitcast(F32).rearrange("p j (b m u) -> p j b u m", m=4, u=2))
+            t = stage.tile([P, PACK, 2, P], F32, name="parted", bufs=PARTED_BUFS, align_bytes=64)
+            nc.vector.tensor_copy(out=t[:].rearrange("p j u (b m) -> p j b u m", m=RUN),
+                                  in_=raw[key[1:]].bitcast(F32).rearrange("p j (b m u) -> p j b u m", m=RUN, u=2))
             parted[key] = t
 
         def turn(key, banks):
@@ -77,10 +92,10 @@ def tile_additive_sylvester_transform_s2_kernel(tc, x, left, right, row_gain, co
             for half in range(2):
                 pt = bank(banks[half])
                 for jj in range(2):
-                    j = 2 * half + jj
+                    piece = 2 * half + jj
                     for u in range(2):
                         q = 2 * jj + u
-                        src = parted[key][:, j, u, :] if key in parted else words[:, j, u:2 * P:2]
+                        src = parted[key][:, piece, u, :] if key in parted else words[:, piece, u:2 * P:2]
                         nc.tensor.transpose(pt[:, q * P:(q + 1) * P], src, ident[:])
                 nc.scalar.copy(
                     out=g_words[:, half * S:(half + 1) * S].rearrange("p (j r u) -> p j r u", j=2, u=2),
@@ -97,15 +112,13 @@ def tile_additive_sylvester_transform_s2_kernel(tc, x, left, right, row_gain, co
             scales[key] = keep.tile([P, S], U8, name="s_" + name, align_bytes=64)
             nc.vector.quantize_mx(out=codes[key][:].bitcast(fmt(key)), scales=scales[key][:], in_=grouped[key][:])
 
-        ring = (4, 5, 6, 0, 1, 2, 3)
-
         def multiply(g, n, j, step, first, last):
             if first:
-                acc[g, n, j] = bank(j if n == 0 else ring[((2 * (n - 1) + g) * PACK + j) % len(ring)])
-            st, _, c = PASSES[step]
-            ks, q = (xt(g, c), j) if st == "x" else (lt(g, j // 2), 2 * (j % 2) + c)
+                acc[g, n, j] = bank(j if n == 0 else RING[((2 * (n - 1) + g) * PACK + j) % len(RING)])
+            matrix, c = PASSES[step][0], PASSES[step][2]
+            ks, piece = (xt(g, c), j) if matrix == "x" else (lt(g, j // 2), 2 * (j % 2) + c)
             km = moving(n, step)
-            cols = slice(q * P, (q + 1) * P)
+            cols = slice(piece * P, (piece + 1) * P)
             nc.tensor.matmul_mx(
                 out=acc[g, n, j][:], lhsT=codes[ks][:, cols].bitcast(fmt(ks)), lhsT_scale=scales[ks][:, cols],
                 rhs=codes[km][:].bitcast(fmt(km)), rhs_scale=scales[km][:], start=first, stop=last)
@@ -149,7 +162,7 @@ def tile_additive_sylvester_transform_s2_kernel(tc, x, left, right, row_gain, co
         load_left(0, 0)
         cols_in = keep.tile([P, 2, 16], BF16, name="cols_in")
         for v, vec in enumerate((col_gain, background)):
-            nc.scalar.dma_start(out=cols_in[:, v, 0:12].rearrange("p (n e) -> p n e", e=PACK),
+            nc.scalar.dma_start(out=cols_in[:, v, 0:W // P].rearrange("p (n e) -> p n e", e=PACK),
                                 in_=vec.rearrange("(n p e) -> p n e", p=P, e=PACK))
         rg = keep.tile([P, 2, PACK], BF16, name="rg")
         nc.scalar.dma_start(out=rg[:], in_=row_gain.rearrange("(g p j) -> p g j", p=P, j=PACK))
@@ -167,7 +180,7 @@ def tile_additive_sylvester_transform_s2_kernel(tc, x, left, right, row_gain, co
         load_left(1, 1)
         load("x", 1, 1, 3)
         for n in (1, 2):
-            for c in range(3):
+            for c in range(W // S):
                 load("right", c, n, n + 1)
 
         col_words = cols_in[:].bitcast(F32)
@@ -186,64 +199,61 @@ def tile_additive_sylvester_transform_s2_kernel(tc, x, left, right, row_gain, co
             return t
 
         rows = [spread(0)]
-
-        A, B = (4, 5), (6, 7)
-        vector, scalar = nc.vector.tensor_copy, nc.scalar.copy
-        turn(lt(0, 0), A)
+        turn(lt(0, 0), PAIR_A)
         rows.append(spread(1))
         weave(moving(0, 0), vector)
-        turn(xt(0, 0), B)
+        turn(xt(0, 0), PAIR_B)
         quantise(lt(0, 0))
-        turn(lt(0, 1), A)
+        turn(lt(0, 1), PAIR_A)
         rows.append(spread(2))
         quantise(moving(0, 0))
-        weave(moving(0, 1), vector, 0, 128)
-        weave(moving(0, 1), scalar, 128, S)
+        weave(moving(0, 1), vector, 0, VECTOR_SHARE_RIGHT00)
+        weave(moving(0, 1), scalar, VECTOR_SHARE_RIGHT00, S)
         quantise(lt(0, 1))
         quantise(xt(0, 0))
         sweep(0, 0, 0, first=True)
-        turn(xt(1, 0), B)
+        turn(xt(1, 0), PAIR_B)
         weave(moving(0, 2), vector)
         quantise(moving(0, 1))
         sweep(0, 0, 1)
-        weave(moving(1, 0), scalar, 0, S // 2)
-        turn(xt(0, 1), A)
+        weave(moving(1, 0), scalar, 0, HALF)
+        turn(xt(0, 1), PAIR_A)
         quantise(moving(0, 2))
         weave(moving(0, 3), vector)
         sweep(0, 0, 2)
-        weave(moving(1, 0), scalar, S // 2, S)
+        weave(moving(1, 0), scalar, HALF, S)
         quantise(xt(1, 0))
-        weave(moving(2, 0), vector, 0, 320)
+        weave(moving(2, 0), vector, 0, VECTOR_SHARE_X02)
         quantise(xt(0, 1))
-        turn(xt(0, 2), B)
+        turn(xt(0, 2), PAIR_B)
         quantise(moving(0, 3))
-        weave(moving(0, 4), vector, 0, 416)
-        weave(moving(0, 4), scalar, 416, S)
+        weave(moving(0, 4), vector)
         sweep(0, 0, 3)
         quantise(xt(0, 2))
         quantise(moving(0, 4))
         quantise(moving(1, 0))
-        turn(lt(1, 0), A)
-        weave(moving(2, 0), vector, 320, S)
-        weave(moving(1, 2), scalar, 0, S // 2)
+        turn(lt(1, 0), PAIR_A)
+        weave(moving(2, 0), scalar, VECTOR_SHARE_X02, S)
         sweep(0, 0, 4, last=True)
-        turn(lt(1, 1), B)
-        weave(moving(1, 2), scalar, S // 2, S)
+
+        turn(lt(1, 1), PAIR_B)
+        weave(moving(1, 2), scalar, 0, HALF)
         drain(0, 0)
         part(xt(1, 1))
         part(xt(1, 2))
         quantise(lt(1, 0))
         quantise(lt(1, 1))
+        weave(moving(1, 2), vector, HALF, S)
         sweep(1, 0, 1, first=True)
-        pt = bank(7)
+        background_bank = bank(BACKGROUND_BANK)
         for n in (1, 2):
             for u in range(2):
-                nc.tensor.transpose(pt[:, (n - 1) * 2 * P + u:n * 2 * P:2], column(1, n, u), ident[:])
-        psum_rows = pt[:].bitcast(BF16)
-        turn(xt(1, 1), A)
-        turn(xt(1, 2), (6, 4))
-        weave(moving(1, 1), vector, 0, 256)
-        weave(moving(1, 1), scalar, 256, S)
+                nc.tensor.transpose(background_bank[:, (n - 1) * 2 * P + u:n * 2 * P:2], column(1, n, u), ident[:])
+        psum_rows = background_bank[:].bitcast(BF16)
+        turn(xt(1, 1), PAIR_A)
+        turn(xt(1, 2), PAIR_LAST)
+        weave(moving(1, 1), vector, 0, HALF)
+        weave(moving(1, 1), scalar, HALF, S)
         quantise(xt(1, 1))
         quantise(xt(1, 2))
         sweep(1, 0, 0)
@@ -253,6 +263,7 @@ def tile_additive_sylvester_transform_s2_kernel(tc, x, left, right, row_gain, co
         quantise(moving(1, 1))
         sweep(1, 0, 3)
         sweep(1, 0, 4, last=True)
+
         for n, step in ((1, 3), (1, 4), (2, 1), (2, 2)):
             weave(moving(n, step), scalar)
         drain(1, 0)
@@ -274,15 +285,16 @@ def tile_additive_sylvester_transform_s2_kernel(tc, x, left, right, row_gain, co
         quantise(moving(2, 4))
         finish(1, 0, 2)
         finish(1, 0, 3)
+
         pass_by_pass(0, 2)
         drain(0, 2)
         tile_by_tile(1, 2)
-        for j in range(2):
+        gain(1, 2, 0)
+        finish(1, 2, 0, nc.gpsimd)
+        for j in (1, 2):
             gain(1, 2, j)
-            finish(1, 2, j, nc.gpsimd)
-        gain(1, 2, 2)
-        finish(1, 2, 2)
-        halves = (slice(0, S // 2), slice(S // 2, S))
+            finish(1, 2, j)
+        halves = (slice(0, HALF), slice(HALF, S))
         for cols in halves:
             gain(1, 2, 3, cols)
         for cols in halves:

from contextlib import ExitStack

import concourse.mybir as mybir
from concourse.masks import make_identity

H, W = 1024, 1536
FLOPS = 2 * H * H * W + 2 * H * W * W

F32 = mybir.dt.float32
BF16 = mybir.dt.bfloat16
U32 = mybir.dt.uint32
U8 = mybir.dt.uint8
E4M3 = mybir.dt.float8_e4m3fn_x4
E5M2 = mybir.dt.float8_e5m2_x4
ALU = mybir.AluOpType

P = 128
PACK = 4
S = P * PACK
HALF = S // 2
RUN = 4

PASSES = (("left", "x", 0), ("x", "right", 0), ("left", "x", 1), ("x", "right", 1), ("x", "right", 2))
STEPS = len(PASSES)

PAIR_A, PAIR_B = (4, 5), (6, 7)
PAIR_LAST = (6, 4)
BACKGROUND_BANK = 7
RING = (4, 5, 6, 0, 1, 2, 3)

STAGE_BUFS = 9
PARTED_BUFS = 2
RESULT_BUFS = 14

VECTOR_SHARE_RIGHT00 = 128
VECTOR_SHARE_X02 = 320


def tile_additive_sylvester_transform_s2_kernel(tc, x, left, right, row_gain, col_gain, background, out):
    nc = tc.nc
    with ExitStack() as ctx:
        keep = ctx.enter_context(tc.tile_pool(name="keep", bufs=1))
        stage = ctx.enter_context(tc.tile_pool(name="stage", bufs=STAGE_BUFS))
        res = ctx.enter_context(tc.tile_pool(name="res", bufs=RESULT_BUFS))
        psum = ctx.enter_context(tc.psum_pool(name="psum", bufs=1))
        ctx.enter_context(tc.manual_schedule())

        raw, parted, grouped, codes, scales, acc, scaled = {}, {}, {}, {}, {}, {}, {}
        vector, scalar = nc.vector.tensor_copy, nc.scalar.copy

        def bank(b):
            return psum.tile([P, S], F32, name="bank%d" % b)

        def moving(n, step):
            return ("moving", PASSES[step][1], PASSES[step][2], n)

        def xt(g, c):
            return ("stationary", "x", g, c)

        def lt(g, h):
            return ("stationary", "left", g, h)

        def load(which, r, c0, c1):
            src = x if which == "x" else right
            t = keep.tile([P, PACK, (c1 - c0) * S], BF16, name="raw_%s%d%d" % (which, r, c0), align_bytes=64)
            nc.sync.dma_start(out=t[:], in_=src[r * S:(r + 1) * S, c0 * S:c1 * S].rearrange("(p j) w -> p j w", j=PACK))
            for c in range(c0, c1):
                raw[which, r, c] = t[:, :, (c - c0) * S:(c - c0 + 1) * S]

        def load_left(g, h):
            t = keep.tile([P, 2, H], BF16, name="raw_left%d%d" % (g, h), align_bytes=64)
            nc.sync.dma_start(out=t[:], in_=left[g * S:(g + 1) * S, :].rearrange("(p j) w -> p j w", j=PACK)[:, 2 * h:2 * h + 2, :])
            raw["left", g, h] = t[:].rearrange("p j (c w) -> p (j c) w", c=2)

        def weave(key, copy, lo=0, hi=S):
            if key not in grouped:
                grouped[key] = stage.tile([P, PACK * S], BF16, name="grouped", align_bytes=64)
            dst = grouped[key][:].rearrange("p (c i t) -> p c t i", i=RUN, t=PACK)
            src = raw[key[1:]].rearrange("p t (c i) -> p c t i", i=RUN)
            copy(out=dst[:, lo // RUN:hi // RUN], in_=src[:, lo // RUN:hi // RUN])

        def part(key):
            t = stage.tile([P, PACK, 2, P], F32, name="parted", bufs=PARTED_BUFS, align_bytes=64)
            nc.vector.tensor_copy(out=t[:].rearrange("p j u (b m) -> p j b u m", m=RUN),
                                  in_=raw[key[1:]].bitcast(F32).rearrange("p j (b m u) -> p j b u m", m=RUN, u=2))
            parted[key] = t

        def turn(key, banks):
            g = stage.tile([P, PACK * S], BF16, name="grouped", align_bytes=64)
            words = raw[key[1:]].bitcast(F32)
            g_words = g[:].bitcast(F32)
            for half in range(2):
                pt = bank(banks[half])
                for jj in range(2):
                    piece = 2 * half + jj
                    for u in range(2):
                        q = 2 * jj + u
                        src = parted[key][:, piece, u, :] if key in parted else words[:, piece, u:2 * P:2]
                        nc.tensor.transpose(pt[:, q * P:(q + 1) * P], src, ident[:])
                nc.scalar.copy(
                    out=g_words[:, half * S:(half + 1) * S].rearrange("p (j r u) -> p j r u", j=2, u=2),
                    in_=pt[:].rearrange("p (j u r) -> p j r u", j=2, u=2),
                )
            grouped[key] = g

        def fmt(key):
            return E5M2 if key[:2] == ("stationary", "x") else E4M3

        def quantise(key):
            name = "%s_%s%d%d" % key
            codes[key] = keep.tile([P, S], U32, name="c_" + name, align_bytes=64)
            scales[key] = keep.tile([P, S], U8, name="s_" + name, align_bytes=64)
            nc.vector.quantize_mx(out=codes[key][:].bitcast(fmt(key)), scales=scales[key][:], in_=grouped[key][:])

        def multiply(g, n, j, step, first, last):
            if first:
                acc[g, n, j] = bank(j if n == 0 else RING[((2 * (n - 1) + g) * PACK + j) % len(RING)])
            matrix, c = PASSES[step][0], PASSES[step][2]
            ks, piece = (xt(g, c), j) if matrix == "x" else (lt(g, j // 2), 2 * (j % 2) + c)
            km = moving(n, step)
            cols = slice(piece * P, (piece + 1) * P)
            nc.tensor.matmul_mx(
                out=acc[g, n, j][:], lhsT=codes[ks][:, cols].bitcast(fmt(ks)), lhsT_scale=scales[ks][:, cols],
                rhs=codes[km][:].bitcast(fmt(km)), rhs_scale=scales[km][:], start=first, stop=last)

        def sweep(g, n, step, first=False, last=False):
            for j in range(PACK):
                multiply(g, n, j, step, first, last)

        def pass_by_pass(g, n):
            for step in range(STEPS):
                sweep(g, n, step, step == 0, step == STEPS - 1)

        def tile_by_tile(g, n):
            for j in range(PACK):
                for step in range(STEPS):
                    multiply(g, n, j, step, step == 0, step == STEPS - 1)

        def gain(g, n, j, cols=slice(0, S)):
            t = res.tile([P, cols.stop - cols.start], F32, name="scaled")
            nc.vector.scalar_tensor_tensor(
                out=t[:], in0=acc[g, n, j][:, cols], scalar=rg[:, g, j:j + 1], in1=rows[n][:, 0, cols],
                op0=ALU.mult, op1=ALU.mult)
            scaled[g, n, j, cols.start] = t

        def finish(g, n, j, engine=nc.vector, cols=slice(0, S)):
            t = scaled[g, n, j, cols.start]
            row = rows[n][:, 1, :] if n == 0 or engine is nc.gpsimd else psum_rows[:, (n - 1) * S:n * S]
            engine.tensor_tensor(out=t[:], in0=t[:], in1=row[:, cols], op=ALU.add)
            dst = out[g * S:(g + 1) * S, n * S:(n + 1) * S].rearrange("(p j) w -> p j w", j=PACK)
            nc.sync.dma_start(out=dst[:, j, cols], in_=t[:])

        def drain(g, n):
            for j in range(PACK):
                gain(g, n, j)
                if j == 0 or (j == 2 and n > 0):
                    finish(g, n, j, nc.gpsimd)
            if n > 0:
                finish(g, n, 1)
                finish(g, n, 3)

        load_left(0, 0)
        cols_in = keep.tile([P, 2, 16], BF16, name="cols_in")
        for v, vec in enumerate((col_gain, background)):
            nc.scalar.dma_start(out=cols_in[:, v, 0:W // P].rearrange("p (n e) -> p n e", e=PACK),
                                in_=vec.rearrange("(n p e) -> p n e", p=P, e=PACK))
        rg = keep.tile([P, 2, PACK], BF16, name="rg")
        nc.scalar.dma_start(out=rg[:], in_=row_gain.rearrange("(g p j) -> p g j", p=P, j=PACK))
        ident = keep.tile([P, P], F32, name="ident")
        make_identity(nc, ident[:])
        load("x", 0, 0, 1)
        load_left(0, 1)
        load("right", 0, 0, 1)
        load("x", 1, 0, 1)
        load("x", 0, 1, 2)
        load("right", 1, 0, 1)
        load("x", 0, 2, 3)
        load("right", 2, 0, 1)
        load_left(1, 0)
        load_left(1, 1)
        load("x", 1, 1, 3)
        for n in (1, 2):
            for c in range(W // S):
                load("right", c, n, n + 1)

        col_words = cols_in[:].bitcast(F32)

        def column(v, n, u):
            return col_words[:, v, 2 * n + u:2 * n + u + 1].to_broadcast([P, P])

        def spread(n):
            pt = bank(n)
            for v in range(2):
                for u in range(2):
                    nc.tensor.transpose(pt[:, (2 * v + u) * P:(2 * v + u + 1) * P], column(v, n, u), ident[:])
            t = keep.tile([P, 2, S], BF16, name="rows%d" % n)
            nc.scalar.copy(out=t[:].bitcast(F32).rearrange("p v (r u) -> p v r u", u=2),
                           in_=pt[:].rearrange("p (v u r) -> p v r u", v=2, u=2))
            return t

        rows = [spread(0)]
        turn(lt(0, 0), PAIR_A)
        rows.append(spread(1))
        weave(moving(0, 0), vector)
        turn(xt(0, 0), PAIR_B)
        quantise(lt(0, 0))
        turn(lt(0, 1), PAIR_A)
        rows.append(spread(2))
        quantise(moving(0, 0))
        weave(moving(0, 1), vector, 0, VECTOR_SHARE_RIGHT00)
        weave(moving(0, 1), scalar, VECTOR_SHARE_RIGHT00, S)
        quantise(lt(0, 1))
        quantise(xt(0, 0))
        sweep(0, 0, 0, first=True)
        turn(xt(1, 0), PAIR_B)
        weave(moving(0, 2), vector)
        quantise(moving(0, 1))
        sweep(0, 0, 1)
        weave(moving(1, 0), scalar, 0, HALF)
        turn(xt(0, 1), PAIR_A)
        quantise(moving(0, 2))
        weave(moving(0, 3), vector)
        sweep(0, 0, 2)
        weave(moving(1, 0), scalar, HALF, S)
        quantise(xt(1, 0))
        weave(moving(2, 0), vector, 0, VECTOR_SHARE_X02)
        quantise(xt(0, 1))
        turn(xt(0, 2), PAIR_B)
        quantise(moving(0, 3))
        weave(moving(0, 4), vector)
        sweep(0, 0, 3)
        quantise(xt(0, 2))
        quantise(moving(0, 4))
        quantise(moving(1, 0))
        turn(lt(1, 0), PAIR_A)
        weave(moving(2, 0), scalar, VECTOR_SHARE_X02, S)
        sweep(0, 0, 4, last=True)

        turn(lt(1, 1), PAIR_B)
        weave(moving(1, 2), scalar, 0, HALF)
        drain(0, 0)
        part(xt(1, 1))
        part(xt(1, 2))
        quantise(lt(1, 0))
        quantise(lt(1, 1))
        weave(moving(1, 2), vector, HALF, S)
        sweep(1, 0, 1, first=True)
        background_bank = bank(BACKGROUND_BANK)
        for n in (1, 2):
            for u in range(2):
                nc.tensor.transpose(background_bank[:, (n - 1) * 2 * P + u:n * 2 * P:2], column(1, n, u), ident[:])
        psum_rows = background_bank[:].bitcast(BF16)
        turn(xt(1, 1), PAIR_A)
        turn(xt(1, 2), PAIR_LAST)
        weave(moving(1, 1), vector, 0, HALF)
        weave(moving(1, 1), scalar, HALF, S)
        quantise(xt(1, 1))
        quantise(xt(1, 2))
        sweep(1, 0, 0)
        sweep(1, 0, 2)
        quantise(moving(2, 0))
        quantise(moving(1, 2))
        quantise(moving(1, 1))
        sweep(1, 0, 3)
        sweep(1, 0, 4, last=True)

        for n, step in ((1, 3), (1, 4), (2, 1), (2, 2)):
            weave(moving(n, step), scalar)
        drain(1, 0)
        quantise(moving(1, 3))
        finish(0, 0, 1)
        finish(0, 0, 2)
        quantise(moving(1, 4))
        pass_by_pass(0, 1)
        finish(0, 0, 3)
        finish(1, 0, 1)
        drain(0, 1)
        for step in (3, 4):
            weave(moving(2, step), scalar)
        quantise(moving(2, 1))
        quantise(moving(2, 2))
        tile_by_tile(1, 1)
        drain(1, 1)
        quantise(moving(2, 3))
        quantise(moving(2, 4))
        finish(1, 0, 2)
        finish(1, 0, 3)

        pass_by_pass(0, 2)
        drain(0, 2)
        tile_by_tile(1, 2)
        gain(1, 2, 0)
        finish(1, 2, 0, nc.gpsimd)
        for j in (1, 2):
            gain(1, 2, j)
            finish(1, 2, j)
        halves = (slice(0, HALF), slice(HALF, S))
        for cols in halves:
            gain(1, 2, 3, cols)
        for cols in halves:
            finish(1, 2, 3, cols=cols)
